import numpy as np
import ml_dtypes


def mxq(x, axis, fmt="e4m3"):
    dtype, down = {"e4m3": (ml_dtypes.float8_e4m3fn, 7), "e5m2": (ml_dtypes.float8_e5m2, 14)}[fmt]
    v = np.moveaxis(np.asarray(x, np.float32).astype(ml_dtypes.bfloat16).astype(np.float64), axis, -1)
    blocks = v.reshape(v.shape[:-1] + (-1, 32))
    amax = np.abs(blocks).max(-1, keepdims=True)
    byte = np.maximum(np.where(amax > 0, np.frexp(amax)[1] - 1 + 127, 0) - down, 1)
    scale = np.exp2(byte - 127.0)
    codes = (blocks / scale).astype(np.float32).astype(dtype).astype(np.float64)
    return np.moveaxis((codes * scale).reshape(v.shape), -1, axis)


WIDE = False


def mx_kscale(k):
    if not WIDE:
        return np.ones(k)
    levels = np.array([10, -10, 5, -5, 0])
    if k % 512:
        return np.exp2(np.random.permutation(np.resize(levels, k // 32))).repeat(32)
    a = np.empty((k // 512, 16))
    for p in range(k // 512):
        a[p, :8] = np.random.permutation(np.resize(levels, 8))
        for g in range(8):
            far = levels[np.abs(levels - a[p, g]) >= 10]
            a[p, g + 8] = far[np.random.randint(len(far))]
    return np.exp2(a.ravel()).repeat(32)


BF16 = ml_dtypes.bfloat16


def bf(x):
    return np.asarray(x, np.float32).astype(BF16)


def f64(x):
    return np.asarray(x).astype(np.float64)

def planes(Y):
    n, m = Y.shape
    b = f64(bf(Y)).reshape(n // 32, 32, m)
    amax = np.abs(b).max(1)
    byte = np.clip(np.where(amax > 0, np.frexp(amax)[1] - 1 + 127 - 7, 1), 1, 254)
    codes = (b * np.exp2(127.0 - byte)[:, None, :]).reshape(n, m).astype(np.float32).astype(ml_dtypes.float8_e4m3fn).view(np.uint8)
    words = codes.reshape(n // 512, 128, 4, m).transpose(0, 1, 3, 2)
    return np.ascontiguousarray(words), np.ascontiguousarray(byte.astype(np.uint8).reshape(n // 512, 16, m))


T, S, C, M, G = 1024, 512, 1024, 1024, 2


def sigmoid(v):
    return 1.0 / (1.0 + np.exp(-v))


def setup_inputs():
    u, t = mx_kscale(S), mx_kscale(C)
    return {
        "s": bf(np.random.standard_normal((T, S)) * u),
        "prev": bf(np.random.standard_normal((T, C))),
        "w1": bf(np.random.standard_normal((S, C)) / np.sqrt(S) / u[:, None]),
        "a": bf(np.random.standard_normal((G, G, C)) / np.sqrt(C)),
        "g": bf((1.0 + 0.1 * np.random.standard_normal(C)) * t),
        "w2": bf(np.random.standard_normal((C, M)) / np.sqrt(C) / t[:, None]),
        "teacher": bf(np.random.standard_normal((T, M)) * 0.7),
    }


def fusion_maps(m, prev, a):
    logits = np.sum(m[:, None, :] * a[0][None, :, :], axis=-1) + np.sum(prev[:, None, :] * a[1][None, :, :], axis=-1)
    return sigmoid(logits)


def core(s, prev, w1, a, g, w2, teacher):
    prev, a, g = f64(prev), f64(a), f64(g)
    m = mxq(f64(s), 1, "e4m3") @ mxq(f64(w1), 0, "e4m3")
    z = fusion_maps(m, prev, a)
    f = g[None, :] * (z[:, 0:1] * m + z[:, 1:2] * prev)
    return (mxq(f, 1, "e4m3") @ mxq(f64(w2), 0, "e4m3")) - f64(teacher)


def reference(s, prev, w1, a, g, w2, teacher):
    R_out = core(s, prev, w1, a, g, w2, teacher)
    words, scales = planes(R_out.T)
    return R_out, words, scales

from contextlib import ExitStack

import concourse.mybir as mybir
from concourse.masks import make_identity

T, S, C, M = 1024, 512, 1024, 1024
FLOPS = 2 * T * S * C + 2 * T * C * M + 2 * 2 * 2 * T * C

F32 = mybir.dt.float32
BF16 = mybir.dt.bfloat16
U32 = mybir.dt.uint32
I32 = mybir.dt.int32
U8 = mybir.dt.uint8
FP8X4 = mybir.dt.float8_e4m3fn_x4
ALU = mybir.AluOpType
ACT = mybir.ActivationFunctionType

P = 128
NT = T // P
H = 512

ACCS, TURNS, SUMS = 4, 2, 1
W1_V = 320
MODE = "VVPPVVPP"
ENG = {"w2":"GGSG","pc":"SS","mc0":"SS","mc1":"SV","mc2":"VS","mc3":"VS","fc":"SS","rc":"SS","U":"SS","TG":"GG","CA":"SV","mode":"VVPPVVPP"}
ORDER = (
    "ab.3 ab.0 abc.3 abc.0 ab.2 abc.2 aT.0 w1v.0 w1s.0 aT.1 aTc.0 ab.1 w1v.1 w1s.1 "
    "w1q.0 abc.1 w1q.1 aTc.1 sT.0 w2i.0 sT.1 sc.0 sc.1 aT.2 aTc.2 PT.0 PT.1 pc.0 "
    "pc.1 gb.1 sq.1 LG.0 w2i.2 sq.0 MT1.1 w2q.0 MT0.1 MT3.1 mc1.1 w2i.1 PT.2 M0.0 "
    "M1.0 VL0.0 mc0.1 pc.2 LM0.1 VL1.0 mc3.1 w2i.3 gbc.1 M1.1 LM1.1 VS.0 VL1.1 SG.0 "
    "U.0 sT.2 ST0.0 sT.3 sc.2 w2q.2 M0.1 sc.3 MT2.1 VL0.1 PT.4 mc2.1 LG.1 pc.4 "
    "gb.0 LM2.1 sq.3 gbc.0 VS.1 sq.2 SG.1 w2q.1 U.1 LM3.1 ST1.0 w2q.3 MT1.3 lgc.1 "
    "ST0.1 TG.0 PT.3 LG.2 ST1.1 pc.3 mc1.3 PT.6 SG.2 U.2 LG.3 TG.1 M0.2 MT3.3 "
    "pc.6 ST0.2 M1.2 M0.4 mc3.3 ST1.2 FT.0 SG.3 MT0.3 VL0.4 U.3 M1.4 TG.2 M0.3 "
    "FT.1 mc0.3 VL1.4 LG.4 fc.1 LM0.3 fc.0 VS.4 ST0.3 SG.4 LM1.3 U.4 QF.0 QF.1 "
    "FT.2 ST0.4 PT.5 fc.2 ST1.4 X0.0 pc.5 QF.2 X0.1 TG.4 SB0.0 X0.2 SB0.1 X1.0 "
    "SB0.2 X1.1 SB1.0 LG.5 M0.5 SB1.1 CA.0 M1.5 M1.3 VL0.5 MT2.3 FT.4 mc2.3 RT.0 "
    "fc.4 VL1.5 LM2.3 rc.0 VS.5 QR.0 LM3.3 SG.5 ST1.3 U.5 CA.1 PT.7 QF.4 lgc.3 "
    "RT.1 ST0.5 TG.3 pc.7 LG.6 ST1.5 rc.1 X1.4 SG.6 U.6 LG.7 SB1.4 X1.2 QR.1 "
    "SG.7 TG.5 M1.6 U.7 SB1.2 X0.4 ST1.6 M0.6 M1.7 CA.2 ST0.6 FT.3 M0.7 ST1.7 "
    "TG.6 fc.3 FT.5 ST0.7 RT.2 SB0.4 fc.5 rc.2 CA.4 QR.2 FT.6 QF.3 QF.5 X0.3 "
    "fc.6 TG.7 X1.3 SB0.3 X1.5 SB1.3 RT.4 SB1.5 X0.5 rc.4 CA.3 FT.7 QR.4 RT.3 "
    "QF.6 fc.7 SB0.5 X0.6 rc.3 QF.7 X1.6 QR.3 SB0.6 X0.7 SB1.6 X1.7 CA.5 CA.6 "
    "SB1.7 RT.5 SB0.7 rc.5 RT.6 CA.7 rc.6 QR.5 RT.7 QR.6 rc.7 QR.7 "
)


def tile_reviewkdattentionfusionteacherresidual_x1_kernel(tc, s, prev, w1, a, g, w2, teacher, out_0, out_1, out_2):
    nc = tc.nc
    with ExitStack() as ctx:
        ctx.enter_context(tc.manual_schedule())
        keep = ctx.enter_context(tc.tile_pool(name="keep", bufs=1))
        work = ctx.enter_context(tc.tile_pool(name="work", bufs=3))
        accs = ctx.enter_context(tc.psum_pool(name="accs", bufs=ACCS))
        zpool = ctx.enter_context(tc.tile_pool(name="zpool", bufs=8))
        pairs = ctx.enter_context(tc.tile_pool(name="pairs", bufs=2))
        stores = ctx.enter_context(tc.tile_pool(name="stores", bufs=4))
        turns = ctx.enter_context(tc.psum_pool(name="turns", bufs=TURNS))
        broad = ctx.enter_context(tc.psum_pool(name="broad", bufs=1))
        sums = ctx.enter_context(tc.psum_pool(name="sums", bufs=SUMS))

        ident = keep.tile([P, P], F32, name="ident")
        make_identity(nc, ident[:])
        ident_b = keep.tile([P, P], BF16, name="ident_b")
        make_identity(nc, ident_b[:])
        warm = keep.tile([P, 1], F32, name="warm")
        nc.vector.memset(warm[:], 0.0)
        nc.scalar.activation(out=warm[:], in_=warm[:], func=ACT.Sigmoid)
        rows = keep.tile([P, C], BF16, name="rows")
        nc.vector.memset(rows[:], 0.0)
        pick = keep.tile([P, P], BF16, name="pick")
        nc.vector.memset(pick[:], 0.0)
        nc.vector.memset(pick[64:65, :], 1.0)
        pick_a = [keep.tile([P, P], BF16, name=f"pick{k}") for k in range(2)]
        for k in range(2):
            nc.vector.memset(pick_a[k][:], 0.0)
            nc.vector.memset(pick_a[k][32 * k : 32 * k + 1, :], 1.0)
        a0t = keep.tile([P, 8, P], F32, name="a0t")
        nc.gpsimd.memset(a0t[:], 0.0)

        s_sb = [keep.tile([P, 2, S], BF16, name=f"s{h}", align_bytes=64) for h in range(4)]
        w1_sb = [keep.tile([P, 4, H], BF16, name=f"w1r{h}", align_bytes=64) for h in range(2)]
        prev_sb = [keep.tile([P, C], BF16, name=f"prev{i}", align_bytes=64) for i in range(NT)]
        w2_sb = [[keep.tile([P, 4, H], BF16, name=f"w2r{h}{k}", align_bytes=64) for k in range(2)] for h in range(2)]
        te_sb = [keep.tile([P, M], BF16, name=f"te{i}", align_bytes=64) for i in range(NT)]

        def load_s(h):
            nc.sync.dma_start(out=s_sb[h][:], in_=s[256 * h : 256 * h + 256, :].rearrange("(i p) k -> p i k", p=P))

        def load_w2(h, k):
            nc.sync.dma_start(out=w2_sb[h][k][:], in_=w2[512 * k : 512 * k + 512, H * h : H * h + H].rearrange("(p j) m -> p j m", j=4))

        def load_rows(tile, src, i):
            nc.sync.dma_start(out=tile[i][:], in_=src[P * i : P * i + P, :])

        nc.scalar.dma_start(out=rows[64:65, :], in_=g.unsqueeze(0))
        nc.scalar.dma_start(out=rows[0:1, :], in_=a[0, 0:1, :])
        nc.scalar.dma_start(out=rows[32:33, :], in_=a[0, 1:2, :])
        nc.scalar.dma_start(out=rows[96:98, :], in_=a[1, :, :])
        load_s(0)
        for h in range(2):
            nc.sync.dma_start(out=w1_sb[h][:], in_=w1[:, H * h : H * h + H].rearrange("(p j) c -> p j c", j=4))
        load_rows(prev_sb, prev, 0)
        load_s(1)
        load_rows(prev_sb, prev, 1)
        for h in range(2):
            for k in range(2):
                load_w2(h, k)
        load_rows(prev_sb, prev, 2)
        load_rows(te_sb, teacher, 0)
        load_s(2)
        load_rows(prev_sb, prev, 3)
        load_rows(te_sb, teacher, 1)
        load_s(3)
        for i in range(4, NT):
            load_rows(prev_sb, prev, i)
            load_rows(te_sb, teacher, i - 2)
        load_rows(te_sb, teacher, NT - 2)
        load_rows(te_sb, teacher, NT - 1)


        def s_of(i):
            w = slice(P * (i % 2), P * (i % 2) + P)
            return t["scod", i // 2][:, w].bitcast(FP8X4), t["sscl", i // 2][:, w]

        def turn_words(words):
            tp = turns.tile([P, 4, P], F32, name="tp")
            for k in range(4):
                nc.tensor.transpose(tp[:, k, :], words[:, P * k : P * k + P], ident[:])
            return tp

        def copy(eng, out, in_):
            if eng == "V":
                nc.vector.tensor_copy(out=out, in_=in_)
            elif eng == "S":
                nc.scalar.copy(out=out, in_=in_)
            else:
                nc.gpsimd.tensor_scalar(out=out, in0=in_, scalar1=1.0, scalar2=0.0, op0=ALU.mult, op1=ALU.add)

        t = {}

        def sT(h):
            words = s_sb[h][:].bitcast(F32)
            tp = turns.tile([P, 2, 2, P], F32, name="tp")
            for i in range(2):
                for u in range(2):
                    nc.tensor.transpose(tp[:, i, u, :], words[:, i, u:256:2], ident[:])
            t["sT", h] = tp

        def sc(h):
            t["sg", h] = work.tile([P, 2, P, 4], BF16, name="sg", align_bytes=64)
            nc.scalar.copy(out=t["sg", h][:].bitcast(F32), in_=t["sT", h][:].rearrange("p i u t -> p i t u"))

        def sq(h):
            t["scod", h] = keep.tile([P, 2 * P], U32, name=f"sc{h}", align_bytes=64)
            t["sscl", h] = keep.tile([P, 2 * P], U8, name=f"ss{h}", align_bytes=64)
            nc.vector.quantize_mx(out=t["scod", h][:].bitcast(FP8X4), scales=t["sscl", h][:], in_=t["sg", h][:].rearrange("p i t j -> p (i t j)"))

        w1g = [keep.tile([P, H, 4], BF16, name=f"w1g{h}", align_bytes=64) for h in range(2)]
        w2g = [keep.tile([P, H, 4], BF16, name=f"w2g{j}", align_bytes=64) for j in range(4)]
        w1q = [(keep.tile([P, H], U32, name=f"w1c{h}", align_bytes=64), keep.tile([P, H], U8, name=f"w1s{h}", align_bytes=64)) for h in range(2)]
        w2q = [(keep.tile([P, H], U32, name=f"w2c{j}", align_bytes=64), keep.tile([P, H], U8, name=f"w2s{j}", align_bytes=64)) for j in range(4)]

        def quant_w(q, grouped):
            nc.vector.quantize_mx(out=q[0][:].bitcast(FP8X4), scales=q[1][:], in_=grouped[:].rearrange("p c j -> p (c j)"))

        def w1v(h):
            copy("V", w1g[h][:, 0:W1_V, :], w1_sb[h][:, :, 0:W1_V].rearrange("p j c -> p c j"))

        def w1s(h):
            copy("S", w1g[h][:, W1_V:H, :], w1_sb[h][:, :, W1_V:H].rearrange("p j c -> p c j"))

        def w1qf(h):
            quant_w(w1q[h], w1g[h])

        def w2i(j):
            copy(ENG["w2"][j], w2g[j][:], w2_sb[j // 2][j % 2][:].rearrange("p j c -> p c j"))

        def w2qf(j):
            quant_w(w2q[j], w2g[j])

        gb = keep.tile([P, C], BF16, name="gb")

        def gbf(h):
            t["gb", h] = turns.tile([P, H], F32, name="tp")
            nc.tensor.matmul(t["gb", h][:], lhsT=pick[:], rhs=rows[:, H * h : H * h + H], start=True, stop=True)

        def gbc(h):
            nc.scalar.copy(out=gb[:, H * h : H * h + H], in_=t["gb", h][:])

        a1t = keep.tile([P, 4, 2], F32, name="a1t")
        a1v = a1t[:].bitcast(BF16).rearrange("p q (k e) -> p q k e", e=2)

        def aT(b):
            if b == 2:
                t["aT", b] = turn_words(rows[:].bitcast(F32))
            else:
                t["aT", b] = turns.tile([P, 4, P], BF16, name="tp")
                for q in range(4):
                    nc.tensor.transpose(t["aT", b][:, q, :], rows[:, P * (4 * b + q) : P * (4 * b + q) + P], ident_b[:])

        def aTc(b):
            if b == 2:
                nc.vector.tensor_copy(out=a1t[:], in_=t["aT", b][:, :, 96:98])
            else:
                nc.vector.tensor_copy(out=a0t[:, 4 * b : 4 * b + 4, 0:2], in_=t["aT", b][:, :, 0:64:32])

        def PT(i):
            t["PT", i] = turn_words(prev_sb[i][:].bitcast(F32))

        def pc(i):
            t["pt", i] = work.tile([P, 4, P], F32, name="pt")
            copy(ENG["pc"][i % 2], t["pt", i][:], t["PT", i][:])

        ab = keep.tile([P, 2, C], BF16, name="ab")

        def abf(j):
            t["ab", j] = turns.tile([P, H], F32, name="tp")
            nc.tensor.matmul(t["ab", j][:], lhsT=pick_a[j // 2][:], rhs=rows[:, H * (j % 2) : H * (j % 2) + H], start=True, stop=True)

        def abc(j):
            nc.scalar.copy(out=ab[:, j // 2, H * (j % 2) : H * (j % 2) + H], in_=t["ab", j][:])

        def MT(p, b):
            acc = accs.tile([P, 2, 2 * P], F32, name="acc")
            for q in range(2):
                w = slice(P * (2 * (b % 2) + q), P * (2 * (b % 2) + q) + P)
                nc.tensor.matmul_mx(acc[:, q, :], lhsT=w1q[b // 2][0][:, w].bitcast(FP8X4), lhsT_scale=w1q[b // 2][1][:, w], rhs=t["scod", p][:].bitcast(FP8X4), rhs_scale=t["sscl", p][:], start=True, stop=True)
            t["MT", p, b] = acc

        def mc(p, b):
            if ("mt", p) not in t:
                t["mt", p] = pairs.tile([P, 8, 2 * P], F32, name="mt")
            copy(ENG[f"mc{b}"][p % 2], t["mt", p][:, 2 * b : 2 * b + 2, :], t["MT", p, b][:])

        def LM(p, b):
            if b == 0:
                t["lm", p] = broad.tile([P, 2 * P], F32, name="lm")
            for q in (2 * b, 2 * b + 1):
                nc.tensor.matmul(t["lm", p][:], lhsT=a0t[:, q, :], rhs=t["mt", p][:, q, :], start=(q == 0), stop=(q == 7))

        def lgc(p):
            t["lgs", p] = pairs.tile([P, 2 * P], F32, name="lgs")
            nc.scalar.copy(out=t["lgs", p][:], in_=t["lm", p][:])

        def LG(i):
            pv = t["pt", i][:].bitcast(BF16).rearrange("p q (t e) -> p q t e", e=2)
            acc = sums.tile([P, 2], F32, name="lg")
            whole = MODE[i] == "P"
            for q in range(4):
                for e in range(2):
                    nc.tensor.matmul(acc[:], lhsT=pv[:, q, :, e], rhs=a1v[:, q, :, e], start=(q == 0 and e == 0), stop=(q == 3 and e == 1 and not whole))
            if whole:
                w = slice(P * (i % 2), P * (i % 2) + P)
                nc.tensor.matmul(acc[:], lhsT=t["lgs", i // 2][:, w], rhs=ident[:, 0:2], start=False, stop=True)
            t["LG", i] = acc

        def VL(i, h):
            if ("part", i) not in t:
                t["part", i] = zpool.tile([P, 2, 2], F32, name="part")
            for k in range(2):
                junk = work.tile([P, H], BF16, name="junk")
                nc.vector.scalar_tensor_tensor(out=junk[:], in0=t["M", i, h][:], scalar=1.0, in1=ab[:, k, H * h : H * h + H], op0=ALU.mult, op1=ALU.mult, accum_out=t["part", i][:, h, k : k + 1])

        def VS(i):
            t["bias", i] = zpool.tile([P, 2], F32, name="bias")
            nc.vector.tensor_tensor(out=t["bias", i][:], in0=t["LG", i][:], in1=t["part", i][:, 0, :], op=ALU.add)

        def SG(i):
            t["z", i] = zpool.tile([P, 2], F32, name="z")
            if MODE[i] == "P":
                nc.scalar.activation(out=t["z", i][:], in_=t["LG", i][:], func=ACT.Sigmoid)
            else:
                for k in range(2):
                    nc.scalar.activation(out=t["z", i][:, k : k + 1], in_=t["part", i][:, 1, k : k + 1], func=ACT.Sigmoid, bias=t["bias", i][:, k : k + 1])

        def M_(i, h):
            cod, scl = s_of(i)
            acc = accs.tile([P, H], F32, name="acc")
            nc.tensor.matmul_mx(acc[:], lhsT=cod, lhsT_scale=scl, rhs=w1q[h][0][:].bitcast(FP8X4), rhs_scale=w1q[h][1][:], start=True, stop=True)
            t["M", i, h] = acc

        def U(i):
            u = t["u", i] = work.tile([P, C], F32, name="u")
            z1 = t["z", i][:, 1:2]
            if ENG["U"][i % 2] == "V":
                nc.vector.tensor_scalar(out=u[:], in0=prev_sb[i][:], scalar1=z1, scalar2=None, op0=ALU.mult)
            elif ENG["U"][i % 2] == "S":
                nc.scalar.activation(out=u[:], in_=prev_sb[i][:], func=ACT.Copy, scale=z1)
            else:
                nc.gpsimd.tensor_scalar(out=u[:], in0=prev_sb[i][:], scalar1=z1, scalar2=0.0, op0=ALU.mult, op1=ALU.add)

        def ST(i, h):
            if ("v", i) not in t:
                t["v", i] = work.tile([P, C], F32, name="v")
            w = slice(H * h, H * h + H)
            nc.vector.scalar_tensor_tensor(out=t["v", i][:, w], in0=t["M", i, h][:], scalar=t["z", i][:, 0:1], in1=t["u", i][:, w], op0=ALU.mult, op1=ALU.add)

        def TG(i):
            t["fb", i] = work.tile([P, 2, 256, 2], BF16, name="fb")
            eng = nc.vector if ENG["TG"][i % 2] == "V" else nc.gpsimd
            eng.tensor_tensor(out=t["fb", i][:], in0=t["v", i][:].rearrange("p (q u e) -> p u q e", u=2, e=2), in1=gb[:].rearrange("p (q u e) -> p u q e", u=2, e=2), op=ALU.mult)

        def FT(i):
            t["FT", i] = turn_words(t["fb", i][:].rearrange("p u q e -> p (u q e)").bitcast(F32))

        def fc(i):
            t["fg", i] = work.tile([P, 2, P, 4], BF16, name="fg", align_bytes=64)
            copy(ENG["fc"][i % 2], t["fg", i][:].bitcast(F32), t["FT", i][:].rearrange("p (u k) t -> p k t u", u=2))

        def QF(i):
            cod = work.tile([P, 2 * P], U32, name="fcod", align_bytes=64)
            scl = work.tile([P, 2 * P], U8, name="fscl", align_bytes=64)
            nc.vector.quantize_mx(out=cod[:].bitcast(FP8X4), scales=scl[:], in_=t["fg", i][:].rearrange("p k t j -> p (k t j)"))
            t["fq", i] = (cod, scl)

        def X(i, h):
            cod, scl = t["fq", i]
            acc = accs.tile([P, H], F32, name="acc")
            for k in range(2):
                x = slice(P * k, P * k + P)
                nc.tensor.matmul_mx(acc[:], lhsT=cod[:, x].bitcast(FP8X4), lhsT_scale=scl[:, x], rhs=w2q[2 * h + k][0][:].bitcast(FP8X4), rhs_scale=w2q[2 * h + k][1][:], start=(k == 0), stop=(k == 1))
            t["X", i, h] = acc

        def SB(i, h):
            if ("r", i) not in t:
                t["r", i] = stores.tile([P, M], F32, name="r")
            w = slice(H * h, H * h + H)
            nc.vector.tensor_tensor(out=t["r", i][:, w], in0=t["X", i, h][:], in1=te_sb[i][:, w], op=ALU.subtract)
            t["sb", i] = t.get(("sb", i), 0) + 1

        def CA(i):
            nc.sync.dma_start(out=out_0[P * i : P * i + P, :], in_=t["r", i][:])
            t["rb", i] = work.tile([P, 2, 256, 2], BF16, name="rb")
            copy(ENG["CA"][i % 2], t["rb", i][:], t["r", i][:].rearrange("p (q u e) -> p u q e", u=2, e=2))

        def RT(i):
            t["RT", i] = turn_words(t["rb", i][:].rearrange("p u q e -> p (u q e)").bitcast(F32))

        def rc(i):
            t["rg", i] = work.tile([P, 2, P, 4], BF16, name="rg", align_bytes=64)
            copy(ENG["rc"][i % 2], t["rg", i][:].bitcast(F32), t["RT", i][:].rearrange("p (u k) t -> p k t u", u=2))

        rs = keep.tile([P, 2, T], U8, name="rs", align_bytes=64)
        words_out = out_1.bitcast(I32).rearrange("k p t o -> p k (t o)")

        def QR(i):
            cod = stores.tile([P, 2, P], U32, name="rcod", align_bytes=64)
            for k in range(2):
                nc.vector.quantize_mx(out=cod[:, k, :].bitcast(FP8X4), scales=rs[:, k, P * i : P * i + P], in_=t["rg", i][:, k, :, :].rearrange("p t j -> p (t j)"))
            nc.sync.dma_start(out=words_out[:, :, P * i : P * i + P], in_=cod[:].bitcast(I32))

        run = dict(PT=PT, pc=pc, LG=LG, SG=SG, U=U, TG=TG, FT=FT, fc=fc, QF=QF, CA=CA, RT=RT, rc=rc, QR=QR, VS=VS, lgc=lgc)
        run.update(sT=sT, sc=sc, sq=sq, w1v=w1v, w1s=w1s, w1q=w1qf, gb=gbf, gbc=gbc, aT=aT, aTc=aTc, w2i=w2i, w2q=w2qf, ab=abf, abc=abc)
        for name, fn, n in (("MT", MT, 4), ("mc", mc, 4), ("LM", LM, 4), ("M", M_, 2), ("ST", ST, 2), ("X", X, 2), ("SB", SB, 2), ("VL", VL, 2)):
            for b in range(n):
                run[f"{name}{b}"] = lambda i, fn=fn, b=b: fn(i, b)
        for item in ORDER.split():
            name, i = item.split(".")
            run[name](int(i))

        scales_out = out_2.bitcast(I32)
        for q in range(4):
            nc.sync.dma_start(out=scales_out[:, 4 * q : 4 * q + 4, :].rearrange("k r t -> r k t"), in_=rs[32 * q : 32 * q + 4, :, :].bitcast(I32))
